import numpy as np
import ml_dtypes


def mxq(x, axis, fmt="e4m3"):
    dtype, down = {"e4m3": (ml_dtypes.float8_e4m3fn, 7), "e5m2": (ml_dtypes.float8_e5m2, 14)}[fmt]
    v = np.moveaxis(np.asarray(x, np.float32).astype(ml_dtypes.bfloat16).astype(np.float64), axis, -1)
    blocks = v.reshape(v.shape[:-1] + (-1, 32))
    amax = np.abs(blocks).max(-1, keepdims=True)
    byte = np.maximum(np.where(amax > 0, np.frexp(amax)[1] - 1 + 127, 0) - down, 1)
    scale = np.exp2(byte - 127.0)
    codes = (blocks / scale).astype(np.float32).astype(dtype).astype(np.float64)
    return np.moveaxis((codes * scale).reshape(v.shape), -1, axis)


WIDE = False


def mx_kscale(k):
    if not WIDE:
        return np.ones(k)
    levels = np.array([10, -10, 5, -5, 0])
    if k % 512:
        return np.exp2(np.random.permutation(np.resize(levels, k // 32))).repeat(32)
    a = np.empty((k // 512, 16))
    for p in range(k // 512):
        a[p, :8] = np.random.permutation(np.resize(levels, 8))
        for g in range(8):
            far = levels[np.abs(levels - a[p, g]) >= 10]
            a[p, g + 8] = far[np.random.randint(len(far))]
    return np.exp2(a.ravel()).repeat(32)


def f64(x):
    return np.asarray(x).astype(np.float64)


def striped(idx):
    return np.tile(idx.reshape(-1, 16).T, (8, 1)).astype(np.uint16)


def unstriped(offs):
    return offs[:16].T.reshape(-1).astype(np.int64)

def planes(y):
    n, m = y.shape
    v = y.astype(np.float32).astype(ml_dtypes.bfloat16).astype(np.float64).reshape(n // 32, 32, m)
    top = np.abs(v).max(1)
    byte = np.clip(np.where(top > 0, np.frexp(top)[1] - 1 + 127 - 7, 1), 1, 254)
    codes = (v * np.exp2(127.0 - byte)[:, None, :]).reshape(n, m).astype(np.float32).astype(ml_dtypes.float8_e4m3fn).view(np.uint8)
    words = codes.reshape(n // 512, 128, 4, m).transpose(0, 1, 3, 2)
    return np.ascontiguousarray(words), np.ascontiguousarray(byte.astype(np.uint8).reshape(n // 512, 16, m))


K, T, S, H = 512, 2048, 1024, 512


def setup_inputs():
    n = np.random.standard_normal
    s = mx_kscale(K)[:, None]
    u = mx_kscale(H)
    return {
        "xT": (n((K, T)) * s).astype(np.float32),
        "w1": (n((K, H)) / np.sqrt(K) / s * u).astype(np.float32),
        "w2": (n((H, H)) / np.sqrt(H) / u[:, None]).astype(np.float32),
        "pos": (0.5 * n((H, S)) * u[:, None]).astype(np.float32),
        "offs": striped(np.random.permutation(T)[(T * np.random.uniform(0, 1, S) ** 4).astype(np.int64)]),
    }


def reference(xT, w1, w2, pos, offs):
    xq = mxq(f64(xT)[:, unstriped(offs)], 0, "e4m3")
    h = (mxq(f64(w1), 0, "e4m3").T @ xq) + f64(pos)
    out_0 = mxq(f64(w2), 0, "e4m3").T @ mxq(h, 0, "e4m3")
    return (out_0,) + planes(out_0)

@@ -1,0 +1,258 @@
+from contextlib import ExitStack
+
+import concourse.mybir as mybir
+
+F32 = mybir.dt.float32
+BF16 = mybir.dt.bfloat16
+U32 = mybir.dt.uint32
+I32 = mybir.dt.int32
+U16 = mybir.dt.uint16
+U8 = mybir.dt.uint8
+FP8X4 = mybir.dt.float8_e4m3fn_x4
+ADD = mybir.AluOpType.add
+
+K, T, S, H = 512, 2048, 1024, 512
+P = 128
+PACK = 4
+CHUNK = 256
+UNIT = 128
+RUN = 4
+SCALAR_UNITS = 6
+FLOPS = 2 * K * H * S + 2 * H * H * S
+
+X_PIECES = [
+    (0, 0, 1024, 1024),
+    (0, 1024, 512, 0),
+    (0, 1536, 512, 160),
+    (1, 0, 1024, 1024),
+    (1, 1024, 512, 0),
+    (1, 1536, 512, 160),
+]
+POS_UNITS = [1, 3, 2, 2]
+H_GROUPS = [1, 1, 2, 2, 1, 1]
+Y_GROUPS = [2, 2, 2, 2]
+STORE_GROUPS = [2, 2, 2, 1, 1]
+X_CHUNKS = [(0, 256), (256, 256), (512, 512)]
+
+
+def tile_picked_embpos_none_lo_kernel(tc, xT, w1, w2, pos, offs, out_0, out_1, out_2):
+    nc = tc.nc
+    n_chunks = S // CHUNK
+    upc = CHUNK // UNIT
+    with ExitStack() as ctx:
+        keep = ctx.enter_context(tc.tile_pool(name="keep", bufs=1))
+        shared = ctx.enter_context(tc.tile_pool(name="shared", bufs=1))
+        ps1 = ctx.enter_context(tc.psum_pool(name="ps1", bufs=4))
+        ps2 = ctx.enter_context(tc.psum_pool(name="ps2", bufs=4))
+
+        x_rows = xT.rearrange("(p j) t -> p j t", j=PACK)
+        pos_rows = pos.rearrange("(p j) s -> p j s", j=PACK)
+        out_rows = out_0.rearrange("(p j) s -> p j s", j=PACK)
+        out_words = out_1.rearrange("z p c r -> p (z c r)").bitcast(I32)
+        out_scales = out_2.rearrange("z q c -> (z q) c").bitcast(I32)
+
+        offsets = keep.tile([P, S // 16], U16, name="offsets")
+
+        x_raw = []
+        for i, (u, c0, width, share) in enumerate(X_PIECES):
+            raw = keep.tile([P, 2, width], F32, name=f"x_raw{i}", align_bytes=64)
+            nc.sync.dma_start(out=raw[:], in_=x_rows[:, 2 * u : 2 * u + 2, c0 : c0 + width])
+            x_raw.append(raw)
+            if i == 0:
+                nc.sync.dma_start(offsets[:], offs)
+
+        def load_w(w, tag):
+            rows = w.rearrange("(p j) c -> p j c", j=PACK)
+            halves = []
+            for a in range(2):
+                raw = keep.tile([P, PACK, H // 2], F32, name=f"{tag}_raw{a}", tag=f"{tag}_raw{a}", align_bytes=64)
+                nc.sync.dma_start(out=raw[:], in_=rows[:, :, a * (H // 2) : (a + 1) * (H // 2)])
+                halves.append(raw)
+            return halves
+
+        w1_raw = load_w(w1, "w1")
+        w2_raw = load_w(w2, "w2")
+        pos_sb = []
+        first = 0
+        for g, count in enumerate(POS_UNITS):
+            tile = keep.tile([P, PACK, count * UNIT], F32, name=f"pos{g}", align_bytes=64)
+            nc.sync.dma_start(out=tile[:], in_=pos_rows[:, :, first * UNIT : (first + count) * UNIT])
+            for a in range(count):
+                pos_sb.append(tile[:, :, a * UNIT : (a + 1) * UNIT])
+            first = first + count
+
+        pairs = [keep.tile([P, T], U32, name=f"pairs{u}", align_bytes=64) for u in range(2)]
+        x_words = [keep.tile([P, CHUNK, 2], U32, name=f"x_words{c}", align_bytes=64) for c in range(2)]
+        x_planes = keep.tile([P, 2, 512], U32, name="x_planes", align_bytes=64)
+
+        def cast_pairs(copy, u, raw, c0, a, b):
+            dst = pairs[u][:, c0 + a : c0 + b].bitcast(BF16).rearrange("p (c i e) -> p c e i", i=RUN, e=2)
+            src = raw[:, :, a:b].rearrange("p e (c i) -> p c e i", i=RUN)
+            copy(out=dst, in_=src)
+
+        def gather(u, c):
+            first, count = X_CHUNKS[c]
+            cols = slice(first // 16, (first + count) // 16)
+            dst = x_words[c][:, :, u] if c < 2 else x_planes[:, u, :]
+            nc.vector.tensor_copy(dst, pairs[u][:].indirect(offsets[:, cols]))
+
+        for i, (u, c0, width, share) in enumerate(X_PIECES):
+            if share > 0:
+                cast_pairs(nc.scalar.copy, u, x_raw[i], c0, 0, share)
+            if share < width:
+                cast_pairs(nc.vector.tensor_copy, u, x_raw[i], c0, share, width)
+            if i == 2:
+                for c in range(3):
+                    gather(0, c)
+
+        def quantize(name, src, width):
+            codes = keep.tile([P, width], U32, name=f"{name}_codes", align_bytes=64)
+            scales = keep.tile([P, width], U8, name=f"{name}_scales", align_bytes=64)
+            nc.vector.quantize_mx(out=codes[:].bitcast(FP8X4), scales=scales[:], in_=src)
+            return codes, scales
+
+        def deal_w(halves, tag):
+            dealt = keep.tile([P, PACK, P, PACK], BF16, name=f"{tag}_bf", tag=f"{tag}_bf", align_bytes=64)
+            for a in range(2):
+                m = slice(a * (P // 2), (a + 1) * (P // 2))
+                nc.scalar.copy(
+                    out=dealt[:, :, m, :].rearrange("p t m j -> p m j t"),
+                    in_=halves[a][:].rearrange("p j (m t) -> p m j t", t=PACK),
+                )
+            return dealt
+
+        def product(bank, w_q, x_q, cols):
+            for t in range(PACK):
+                m = slice(t * P, (t + 1) * P)
+                nc.tensor.matmul_mx(
+                    out=bank[:, t, :],
+                    lhsT=w_q[0][:, m].bitcast(FP8X4),
+                    lhsT_scale=w_q[1][:, m],
+                    rhs=x_q[0][:, cols].bitcast(FP8X4),
+                    rhs_scale=x_q[1][:, cols],
+                    start=True,
+                    stop=True,
+                )
+
+        w1_bf = deal_w(w1_raw, "w1")
+        w2_bf = deal_w(w2_raw, "w2")
+
+        x_q = {}
+
+        def x_in(c):
+            return x_words[c][:].rearrange("p n u -> p (n u)").bitcast(BF16)
+
+        y_codes = keep.tile([P, S], U32, name="y_codes", align_bytes=64)
+        y_scales = keep.tile([P, S], U8, name="y_scales", align_bytes=64)
+
+        gather(1, 0)
+        gather(1, 1)
+        x_q[0] = quantize("x0", x_in(0), CHUNK)
+        w1_q = quantize("w1", w1_bf[:].rearrange("p t m j -> p (t m j)"), H)
+        gather(1, 2)
+        late_codes = keep.tile([P, CHUNK], U32, name="late_codes", tag="w1_bf", align_bytes=64)
+        late_scales = keep.tile([P, CHUNK], U8, name="late_scales", align_bytes=64)
+        nc.vector.quantize_mx(out=late_codes[:].bitcast(FP8X4), scales=late_scales[:], in_=x_in(1))
+        x_q[1] = (late_codes, late_scales)
+        woven = keep.tile([P, 512, 2], U32, name="woven", tag="w2_raw1", align_bytes=64)
+        nc.scalar.copy(
+            out=woven[:].rearrange("p (c i) u -> p c u i", i=RUN),
+            in_=x_planes[:].rearrange("p u (c i) -> p c u i", i=RUN),
+        )
+
+        def groups(counts):
+            where = []
+            first = 0
+            for g, count in enumerate(counts):
+                for a in range(count):
+                    where.append((g, a, count, first))
+                first = first + count
+            return where
+
+        h_at = groups(H_GROUPS)
+        y_at = groups(Y_GROUPS)
+        store_at = groups(STORE_GROUPS)
+        h_bf = {}
+        h_q = {}
+        y_f32 = {}
+        y_bf = {}
+
+        def layer1(n):
+            c = min(n // 2, 2)
+            a = n - 2 * c
+            bank = ps1.tile([P, PACK, UNIT], F32, name="bank1")
+            product(bank, w1_q, x_q[c], slice(a * UNIT, (a + 1) * UNIT))
+            g, a, count, first = h_at[n]
+            if a == 0:
+                h_bf[g] = keep.tile([P, count * UNIT, PACK], BF16, name=f"h_bf{g}", align_bytes=64)
+            nc.vector.tensor_tensor(
+                h_bf[g][:, a * UNIT : (a + 1) * UNIT, :].rearrange("p (c i) t -> p c t i", i=RUN),
+                bank[:].rearrange("p t (c i) -> p c t i", i=RUN),
+                pos_sb[n].rearrange("p t (c i) -> p c t i", i=RUN),
+                ADD,
+            )
+
+        def h_quant(g):
+            h_q[g] = quantize(f"h{g}", h_bf[g][:].rearrange("p n t -> p (n t)"), H_GROUPS[g] * UNIT)
+
+        def store_scales(tok0, tok1, queues):
+            for q in range(4):
+                queues[q % len(queues)].dma_start(
+                    out=out_scales[4 * q : 4 * q + 4, tok0 // 4 : tok1 // 4],
+                    in_=y_scales[32 * q : 32 * q + 4, tok0:tok1].bitcast(I32),
+                )
+
+        n_units = S // UNIT
+
+        def layer2(n, w2_q):
+            hg, ha, hcount, hfirst = h_at[n]
+            g, a, count, first = y_at[n]
+            sg, sa, scount, sfirst = store_at[n]
+            if a == 0:
+                y_bf[g] = keep.tile([P, count * UNIT, PACK], BF16, name=f"y_bf{g}", align_bytes=64)
+            if sa == 0:
+                y_f32[sg] = keep.tile([P, PACK, scount * UNIT], F32, name=f"y_f32{sg}", align_bytes=64)
+            bank = ps2.tile([P, PACK, UNIT], F32, name="bank2")
+            product(bank, w2_q, h_q[hg], slice(ha * UNIT, (ha + 1) * UNIT))
+            y_cols = y_f32[sg][:, :, sa * UNIT : (sa + 1) * UNIT]
+            dst = y_bf[g][:, a * UNIT : (a + 1) * UNIT, :].rearrange("p (c i) t -> p c t i", i=RUN)
+            from_bank = bank[:].rearrange("p t (c i) -> p c t i", i=RUN)
+            if n == n_units - 1:
+                nc.vector.tensor_copy(out=dst, in_=from_bank)
+            nc.scalar.copy(out=y_cols, in_=bank[:])
+            if n < SCALAR_UNITS:
+                nc.scalar.copy(out=dst, in_=from_bank)
+            elif n < n_units - 1:
+                nc.vector.tensor_copy(out=dst, in_=y_cols.rearrange("p t (c i) -> p c t i", i=RUN))
+            if sa == scount - 1:
+                tok = slice(sfirst * UNIT, (sfirst + scount) * UNIT)
+                nc.sync.dma_start(out=out_rows[:, :, tok], in_=y_f32[sg][:])
+
+        def y_quant(g):
+            first = sum(Y_GROUPS[:g])
+            tok = slice(first * UNIT, (first + Y_GROUPS[g]) * UNIT)
+            nc.vector.quantize_mx(
+                out=y_codes[:, tok].bitcast(FP8X4),
+                scales=y_scales[:, tok],
+                in_=y_bf[g][:].rearrange("p n t -> p (n t)"),
+            )
+            if g % 2 == 1:
+                tok = slice((first - 2) * UNIT, (first + 2) * UNIT)
+                nc.sync.dma_start(out=out_words[:, tok], in_=y_codes[:, tok].bitcast(I32))
+
+        layer1(0)
+        w2_q = quantize("w2", w2_bf[:].rearrange("p t m j -> p (t m j)"), H)
+        h_quant(0)
+        layer2(0, w2_q)
+        for n in range(1, n_units):
+            layer1(n)
+            if n == 1:
+                x_q[2] = quantize("x2", woven[:].rearrange("p n u -> p (n u)").bitcast(BF16), 512)
+            g, a, count, first = h_at[n]
+            if a == count - 1:
+                h_quant(g)
+                for m in range(first, first + count):
+                    layer2(m, w2_q)
+        for g in range(len(Y_GROUPS)):
+            y_quant(g)
+        store_scales(0, S, [nc.sync, nc.scalar])

@@ -14,34 +14,34 @@ ADD = mybir.AluOpType.add
 K, T, S, H = 512, 2048, 1024, 512
 P = 128
 PACK = 4
-CHUNK = 256
 UNIT = 128
 RUN = 4
-SCALAR_UNITS = 6
 FLOPS = 2 * K * H * S + 2 * H * H * S
 
-X_PIECES = [
-    (0, 0, 1024, 1024),
-    (0, 1024, 512, 0),
-    (0, 1536, 512, 160),
-    (1, 0, 1024, 1024),
-    (1, 1024, 512, 0),
-    (1, 1536, 512, 160),
-]
-POS_UNITS = [1, 3, 2, 2]
-H_GROUPS = [1, 1, 2, 2, 1, 1]
-Y_GROUPS = [2, 2, 2, 2]
-STORE_GROUPS = [2, 2, 2, 1, 1]
+X_PIECES = [(0, 0, 2048, 672), (1, 0, 1024, 1024), (1, 1024, 1024, 336)]
 X_CHUNKS = [(0, 256), (256, 256), (512, 512)]
+POS_UNITS = [2, 2, 4]
+H_GROUPS = [2, 2, 2, 1, 1]
+STORE_GROUPS = [2, 2, 2, 2]
+SCALAR_ROUNDS = (0, 1, 6, 7)
+Y_GROUP = 2
+
+
+def groups(counts):
+    where = []
+    first = 0
+    for g, count in enumerate(counts):
+        for a in range(count):
+            where.append((g, a, count, first))
+        first = first + count
+    return where
 
 
 def tile_picked_embpos_none_lo_kernel(tc, xT, w1, w2, pos, offs, out_0, out_1, out_2):
     nc = tc.nc
-    n_chunks = S // CHUNK
-    upc = CHUNK // UNIT
+    n_units = S // UNIT
     with ExitStack() as ctx:
         keep = ctx.enter_context(tc.tile_pool(name="keep", bufs=1))
-        shared = ctx.enter_context(tc.tile_pool(name="shared", bufs=1))
         ps1 = ctx.enter_context(tc.psum_pool(name="ps1", bufs=4))
         ps2 = ctx.enter_context(tc.psum_pool(name="ps2", bufs=4))
 
@@ -62,27 +62,21 @@ def tile_picked_embpos_none_lo_kernel(tc, xT, w1, w2, pos, offs, out_0, out_1, o
                 nc.sync.dma_start(offsets[:], offs)
 
         def load_w(w, tag):
-            rows = w.rearrange("(p j) c -> p j c", j=PACK)
-            halves = []
-            for a in range(2):
-                raw = keep.tile([P, PACK, H // 2], F32, name=f"{tag}_raw{a}", tag=f"{tag}_raw{a}", align_bytes=64)
-                nc.sync.dma_start(out=raw[:], in_=rows[:, :, a * (H // 2) : (a + 1) * (H // 2)])
-                halves.append(raw)
-            return halves
+            raw = keep.tile([P, PACK, H], F32, name=tag, tag=tag, align_bytes=64)
+            nc.sync.dma_start(out=raw[:], in_=w.rearrange("(p j) c -> p j c", j=PACK))
+            return raw
 
-        w1_raw = load_w(w1, "w1")
-        w2_raw = load_w(w2, "w2")
+        w1_raw = load_w(w1, "w1_raw")
+        w2_raw = load_w(w2, "w2_raw")
         pos_sb = []
-        first = 0
-        for g, count in enumerate(POS_UNITS):
-            tile = keep.tile([P, PACK, count * UNIT], F32, name=f"pos{g}", align_bytes=64)
-            nc.sync.dma_start(out=tile[:], in_=pos_rows[:, :, first * UNIT : (first + count) * UNIT])
-            for a in range(count):
-                pos_sb.append(tile[:, :, a * UNIT : (a + 1) * UNIT])
-            first = first + count
+        for g, a, count, first in groups(POS_UNITS):
+            if a == 0:
+                pos_tile = keep.tile([P, PACK, count * UNIT], F32, name=f"pos{g}", align_bytes=64)
+                nc.sync.dma_start(out=pos_tile[:], in_=pos_rows[:, :, first * UNIT : (first + count) * UNIT])
+            pos_sb.append(pos_tile[:, :, a * UNIT : (a + 1) * UNIT])
 
         pairs = [keep.tile([P, T], U32, name=f"pairs{u}", align_bytes=64) for u in range(2)]
-        x_words = [keep.tile([P, CHUNK, 2], U32, name=f"x_words{c}", align_bytes=64) for c in range(2)]
+        x_words = [keep.tile([P, 256, 2], U32, name=f"x_words{c}", align_bytes=64) for c in range(2)]
         x_planes = keep.tile([P, 2, 512], U32, name="x_planes", align_bytes=64)
 
         def cast_pairs(copy, u, raw, c0, a, b):
@@ -101,7 +95,7 @@ def tile_picked_embpos_none_lo_kernel(tc, xT, w1, w2, pos, offs, out_0, out_1, o
                 cast_pairs(nc.scalar.copy, u, x_raw[i], c0, 0, share)
             if share < width:
                 cast_pairs(nc.vector.tensor_copy, u, x_raw[i], c0, share, width)
-            if i == 2:
+            if u == 0 and c0 + width == T:
                 for c in range(3):
                     gather(0, c)
 
@@ -111,15 +105,13 @@ def tile_picked_embpos_none_lo_kernel(tc, xT, w1, w2, pos, offs, out_0, out_1, o
             nc.vector.quantize_mx(out=codes[:].bitcast(FP8X4), scales=scales[:], in_=src)
             return codes, scales
 
-        def deal_w(halves, tag):
-            dealt = keep.tile([P, PACK, P, PACK], BF16, name=f"{tag}_bf", tag=f"{tag}_bf", align_bytes=64)
-            for a in range(2):
-                m = slice(a * (P // 2), (a + 1) * (P // 2))
-                nc.scalar.copy(
-                    out=dealt[:, :, m, :].rearrange("p t m j -> p m j t"),
-                    in_=halves[a][:].rearrange("p j (m t) -> p m j t", t=PACK),
-                )
-            return dealt
+        def deal_w(raw, tag):
+            dealt = keep.tile([P, PACK, P, PACK], BF16, name=tag, align_bytes=64)
+            nc.scalar.copy(
+                out=dealt[:].rearrange("p t m j -> p m j t"),
+                in_=raw[:].rearrange("p j (m t) -> p m j t", t=PACK),
+            )
+            return dealt[:].rearrange("p t m j -> p (t m j)")
 
         def product(bank, w_q, x_q, cols):
             for t in range(PACK):
@@ -134,48 +126,36 @@ def tile_picked_embpos_none_lo_kernel(tc, xT, w1, w2, pos, offs, out_0, out_1, o
                     stop=True,
                 )
 
-        w1_bf = deal_w(w1_raw, "w1")
-        w2_bf = deal_w(w2_raw, "w2")
+        def as_bf16(words):
+            return words[:].rearrange("p n u -> p (n u)").bitcast(BF16)
 
-        x_q = {}
-
-        def x_in(c):
-            return x_words[c][:].rearrange("p n u -> p (n u)").bitcast(BF16)
+        w1_bf = deal_w(w1_raw, "w1_bf")
+        w2_bf = deal_w(w2_raw, "w2_bf")
 
         y_codes = keep.tile([P, S], U32, name="y_codes", align_bytes=64)
         y_scales = keep.tile([P, S], U8, name="y_scales", align_bytes=64)
 
+        x_q = {}
         gather(1, 0)
         gather(1, 1)
-        x_q[0] = quantize("x0", x_in(0), CHUNK)
-        w1_q = quantize("w1", w1_bf[:].rearrange("p t m j -> p (t m j)"), H)
+        x_q[0] = quantize("x0", as_bf16(x_words[0]), 256)
+        w1_q = quantize("w1", w1_bf, H)
         gather(1, 2)
-        late_codes = keep.tile([P, CHUNK], U32, name="late_codes", tag="w1_bf", align_bytes=64)
-        late_scales = keep.tile([P, CHUNK], U8, name="late_scales", align_bytes=64)
-        nc.vector.quantize_mx(out=late_codes[:].bitcast(FP8X4), scales=late_scales[:], in_=x_in(1))
-        x_q[1] = (late_codes, late_scales)
-        woven = keep.tile([P, 512, 2], U32, name="woven", tag="w2_raw1", align_bytes=64)
+        x_q[1] = quantize("x1", as_bf16(x_words[1]), 256)
+        woven = keep.tile([P, 512, 2], U32, name="woven", tag="w2_raw", align_bytes=64)
         nc.scalar.copy(
             out=woven[:].rearrange("p (c i) u -> p c u i", i=RUN),
             in_=x_planes[:].rearrange("p u (c i) -> p c u i", i=RUN),
         )
 
-        def groups(counts):
-            where = []
-            first = 0
-            for g, count in enumerate(counts):
-                for a in range(count):
-                    where.append((g, a, count, first))
-                first = first + count
-            return where
-
         h_at = groups(H_GROUPS)
-        y_at = groups(Y_GROUPS)
         store_at = groups(STORE_GROUPS)
         h_bf = {}
         h_q = {}
         y_f32 = {}
-        y_bf = {}
+        y_cols = {}
+        banks = {}
+        y_bf = [keep.tile([P, Y_GROUP * UNIT, PACK], BF16, name=f"y_bf{g}", align_bytes=64) for g in range(n_units // Y_GROUP)]
 
         def layer1(n):
             c = min(n // 2, 2)
@@ -192,67 +172,57 @@ def tile_picked_embpos_none_lo_kernel(tc, xT, w1, w2, pos, offs, out_0, out_1, o
                 ADD,
             )
 
-        def h_quant(g):
-            h_q[g] = quantize(f"h{g}", h_bf[g][:].rearrange("p n t -> p (n t)"), H_GROUPS[g] * UNIT)
-
-        def store_scales(tok0, tok1, queues):
-            for q in range(4):
-                queues[q % len(queues)].dma_start(
-                    out=out_scales[4 * q : 4 * q + 4, tok0 // 4 : tok1 // 4],
-                    in_=y_scales[32 * q : 32 * q + 4, tok0:tok1].bitcast(I32),
-                )
-
-        n_units = S // UNIT
-
-        def layer2(n, w2_q):
+        def layer2(n):
             hg, ha, hcount, hfirst = h_at[n]
-            g, a, count, first = y_at[n]
             sg, sa, scount, sfirst = store_at[n]
-            if a == 0:
-                y_bf[g] = keep.tile([P, count * UNIT, PACK], BF16, name=f"y_bf{g}", align_bytes=64)
             if sa == 0:
                 y_f32[sg] = keep.tile([P, PACK, scount * UNIT], F32, name=f"y_f32{sg}", align_bytes=64)
             bank = ps2.tile([P, PACK, UNIT], F32, name="bank2")
             product(bank, w2_q, h_q[hg], slice(ha * UNIT, (ha + 1) * UNIT))
-            y_cols = y_f32[sg][:, :, sa * UNIT : (sa + 1) * UNIT]
-            dst = y_bf[g][:, a * UNIT : (a + 1) * UNIT, :].rearrange("p (c i) t -> p c t i", i=RUN)
-            from_bank = bank[:].rearrange("p t (c i) -> p c t i", i=RUN)
-            if n == n_units - 1:
-                nc.vector.tensor_copy(out=dst, in_=from_bank)
-            nc.scalar.copy(out=y_cols, in_=bank[:])
-            if n < SCALAR_UNITS:
-                nc.scalar.copy(out=dst, in_=from_bank)
-            elif n < n_units - 1:
-                nc.vector.tensor_copy(out=dst, in_=y_cols.rearrange("p t (c i) -> p c t i", i=RUN))
+            banks[n] = bank
+            y_cols[n] = y_f32[sg][:, :, sa * UNIT : (sa + 1) * UNIT]
+            nc.scalar.copy(out=y_cols[n], in_=bank[:])
             if sa == scount - 1:
                 tok = slice(sfirst * UNIT, (sfirst + scount) * UNIT)
                 nc.sync.dma_start(out=out_rows[:, :, tok], in_=y_f32[sg][:])
 
+        def y_round(n):
+            g, a = divmod(n, Y_GROUP)
+            dst = y_bf[g][:, a * UNIT : (a + 1) * UNIT, :]
+            if n in SCALAR_ROUNDS:
+                nc.scalar.copy(out=dst, in_=banks[n][:].rearrange("p t n -> p n t"))
+            else:
+                nc.vector.tensor_copy(
+                    out=dst.rearrange("p (c i) t -> p c t i", i=RUN),
+                    in_=y_cols[n].rearrange("p t (c i) -> p c t i", i=RUN),
+                )
+
         def y_quant(g):
-            first = sum(Y_GROUPS[:g])
-            tok = slice(first * UNIT, (first + Y_GROUPS[g]) * UNIT)
+            tok = slice(g * Y_GROUP * UNIT, (g + 1) * Y_GROUP * UNIT)
             nc.vector.quantize_mx(
                 out=y_codes[:, tok].bitcast(FP8X4),
                 scales=y_scales[:, tok],
                 in_=y_bf[g][:].rearrange("p n t -> p (n t)"),
             )
-            if g % 2 == 1:
-                tok = slice((first - 2) * UNIT, (first + 2) * UNIT)
-                nc.sync.dma_start(out=out_words[:, tok], in_=y_codes[:, tok].bitcast(I32))
+            nc.sync.dma_start(out=out_words[:, tok], in_=y_codes[:, tok].bitcast(I32))
 
-        layer1(0)
-        w2_q = quantize("w2", w2_bf[:].rearrange("p t m j -> p (t m j)"), H)
-        h_quant(0)
-        layer2(0, w2_q)
-        for n in range(1, n_units):
+        w2_q = quantize("w2", w2_bf, H)
+        for n in range(n_units):
             layer1(n)
-            if n == 1:
-                x_q[2] = quantize("x2", woven[:].rearrange("p n u -> p (n u)").bitcast(BF16), 512)
             g, a, count, first = h_at[n]
             if a == count - 1:
-                h_quant(g)
+                h_q[g] = quantize(f"h{g}", h_bf[g][:].rearrange("p n t -> p (n t)"), count * UNIT)
                 for m in range(first, first + count):
-                    layer2(m, w2_q)
-        for g in range(len(Y_GROUPS)):
+                    layer2(m)
+            if n == 1:
+                x_q[2] = quantize("x2", as_bf16(woven), 512)
+                y_round(0)
+                y_round(1)
+                y_quant(0)
+        for g in range(1, n_units // Y_GROUP):
+            for a in range(Y_GROUP):
+                y_round(g * Y_GROUP + a)
             y_quant(g)
-        store_scales(0, S, [nc.sync, nc.scalar])
+        for q in range(4):
+            queue = nc.sync if q % 2 == 0 else nc.scalar
+            queue.dma_start(out=out_scales[4 * q : 4 * q + 4, :], in_=y_scales[32 * q : 32 * q + 4, :].bitcast(I32))

@@ -18,13 +18,13 @@ UNIT = 128
 RUN = 4
 FLOPS = 2 * K * H * S + 2 * H * H * S
 
-X_PIECES = [(0, 0, 2048, 672), (1, 0, 1024, 1024), (1, 1024, 1024, 336)]
+X_PIECES = [(0, 0, 1024, 1024), (0, 1024, 1024, 336), (1, 0, 1024, 1024), (1, 1024, 512, 0), (1, 1536, 512, 160)]
 X_CHUNKS = [(0, 256), (256, 256), (512, 512)]
-POS_UNITS = [2, 2, 4]
+POS_UNITS = [1, 1, 2, 4]
 H_GROUPS = [2, 2, 2, 1, 1]
-STORE_GROUPS = [2, 2, 2, 2]
-SCALAR_ROUNDS = (0, 1, 6, 7)
-Y_GROUP = 2
+STORE_GROUPS = [1, 1, 1, 1, 1, 1, 1, 1]
+SCALAR_ROUNDS = (0, 1, 7)
+Y_GROUPS = [2, 4, 2]
 
 
 def groups(counts):
@@ -62,9 +62,13 @@ def tile_picked_embpos_none_lo_kernel(tc, xT, w1, w2, pos, offs, out_0, out_1, o
                 nc.sync.dma_start(offsets[:], offs)
 
         def load_w(w, tag):
-            raw = keep.tile([P, PACK, H], F32, name=tag, tag=tag, align_bytes=64)
-            nc.sync.dma_start(out=raw[:], in_=w.rearrange("(p j) c -> p j c", j=PACK))
-            return raw
+            rows = w.rearrange("(p j) c -> p j c", j=PACK)
+            halves = []
+            for a in range(2):
+                raw = keep.tile([P, PACK, H // 2], F32, name=f"{tag}{a}", tag=f"{tag}{a}", align_bytes=64)
+                nc.sync.dma_start(out=raw[:], in_=rows[:, :, a * (H // 2) : (a + 1) * (H // 2)])
+                halves.append(raw)
+            return halves
 
         w1_raw = load_w(w1, "w1_raw")
         w2_raw = load_w(w2, "w2_raw")
@@ -99,18 +103,19 @@ def tile_picked_embpos_none_lo_kernel(tc, xT, w1, w2, pos, offs, out_0, out_1, o
                 for c in range(3):
                     gather(0, c)
 
-        def quantize(name, src, width):
-            codes = keep.tile([P, width], U32, name=f"{name}_codes", align_bytes=64)
+        def quantize(name, src, width, tag=""):
+            codes = keep.tile([P, width], U32, name=f"{name}_codes", tag=tag, align_bytes=64)
             scales = keep.tile([P, width], U8, name=f"{name}_scales", align_bytes=64)
             nc.vector.quantize_mx(out=codes[:].bitcast(FP8X4), scales=scales[:], in_=src)
             return codes, scales
 
         def deal_w(raw, tag):
-            dealt = keep.tile([P, PACK, P, PACK], BF16, name=tag, align_bytes=64)
-            nc.scalar.copy(
-                out=dealt[:].rearrange("p t m j -> p m j t"),
-                in_=raw[:].rearrange("p j (m t) -> p m j t", t=PACK),
-            )
+            dealt = keep.tile([P, PACK, P, PACK], BF16, name=tag, tag=tag, align_bytes=64)
+            for a in range(2):
+                nc.scalar.copy(
+                    out=dealt[:, :, a * (P // 2) : (a + 1) * (P // 2), :].rearrange("p t m j -> p m j t"),
+                    in_=raw[a][:].rearrange("p j (m t) -> p m j t", t=PACK),
+                )
             return dealt[:].rearrange("p t m j -> p (t m j)")
 
         def product(bank, w_q, x_q, cols):
@@ -141,8 +146,8 @@ def tile_picked_embpos_none_lo_kernel(tc, xT, w1, w2, pos, offs, out_0, out_1, o
         x_q[0] = quantize("x0", as_bf16(x_words[0]), 256)
         w1_q = quantize("w1", w1_bf, H)
         gather(1, 2)
-        x_q[1] = quantize("x1", as_bf16(x_words[1]), 256)
-        woven = keep.tile([P, 512, 2], U32, name="woven", tag="w2_raw", align_bytes=64)
+        x_q[1] = quantize("x1", as_bf16(x_words[1]), 256, "w1_bf")
+        woven = keep.tile([P, 512, 2], U32, name="woven", tag="w2_raw1", align_bytes=64)
         nc.scalar.copy(
             out=woven[:].rearrange("p (c i) u -> p c u i", i=RUN),
             in_=x_planes[:].rearrange("p u (c i) -> p c u i", i=RUN),
@@ -155,7 +160,8 @@ def tile_picked_embpos_none_lo_kernel(tc, xT, w1, w2, pos, offs, out_0, out_1, o
         y_f32 = {}
         y_cols = {}
         banks = {}
-        y_bf = [keep.tile([P, Y_GROUP * UNIT, PACK], BF16, name=f"y_bf{g}", align_bytes=64) for g in range(n_units // Y_GROUP)]
+        y_at = groups(Y_GROUPS)
+        y_bf = [keep.tile([P, count * UNIT, PACK], BF16, name=f"y_bf{g}", align_bytes=64) for g, count in enumerate(Y_GROUPS)]
 
         def layer1(n):
             c = min(n // 2, 2)
@@ -187,7 +193,7 @@ def tile_picked_embpos_none_lo_kernel(tc, xT, w1, w2, pos, offs, out_0, out_1, o
                 nc.sync.dma_start(out=out_rows[:, :, tok], in_=y_f32[sg][:])
 
         def y_round(n):
-            g, a = divmod(n, Y_GROUP)
+            g, a, count, first = y_at[n]
             dst = y_bf[g][:, a * UNIT : (a + 1) * UNIT, :]
             if n in SCALAR_ROUNDS:
                 nc.scalar.copy(out=dst, in_=banks[n][:].rearrange("p t n -> p n t"))
@@ -198,7 +204,8 @@ def tile_picked_embpos_none_lo_kernel(tc, xT, w1, w2, pos, offs, out_0, out_1, o
                 )
 
         def y_quant(g):
-            tok = slice(g * Y_GROUP * UNIT, (g + 1) * Y_GROUP * UNIT)
+            first = sum(Y_GROUPS[:g])
+            tok = slice(first * UNIT, (first + Y_GROUPS[g]) * UNIT)
             nc.vector.quantize_mx(
                 out=y_codes[:, tok].bitcast(FP8X4),
                 scales=y_scales[:, tok],
@@ -219,10 +226,11 @@ def tile_picked_embpos_none_lo_kernel(tc, xT, w1, w2, pos, offs, out_0, out_1, o
                 y_round(0)
                 y_round(1)
                 y_quant(0)
-        for g in range(1, n_units // Y_GROUP):
-            for a in range(Y_GROUP):
-                y_round(g * Y_GROUP + a)
-            y_quant(g)
+        for n in range(Y_GROUPS[0], n_units):
+            y_round(n)
+            g, a, count, first = y_at[n]
+            if a == count - 1:
+                y_quant(g)
         for q in range(4):
             queue = nc.sync if q % 2 == 0 else nc.scalar
             queue.dma_start(out=out_scales[4 * q : 4 * q + 4, :], in_=y_scales[32 * q : 32 * q + 4, :].bitcast(I32))

@@ -12,225 +12,231 @@ FP8X4 = mybir.dt.float8_e4m3fn_x4
 ADD = mybir.AluOpType.add
 
 K, T, S, H = 512, 2048, 1024, 512
-P = 128
-PACK = 4
-UNIT = 128
-RUN = 4
 FLOPS = 2 * K * H * S + 2 * H * H * S
 
-X_PIECES = [(0, 0, 1024, 1024), (0, 1024, 1024, 336), (1, 0, 1024, 1024), (1, 1024, 512, 0), (1, 1536, 512, 160)]
-X_CHUNKS = [(0, 256), (256, 256), (512, 512)]
-POS_UNITS = [1, 1, 2, 4]
-H_GROUPS = [2, 2, 2, 1, 1]
-STORE_GROUPS = [1, 1, 1, 1, 1, 1, 1, 1]
-SCALAR_ROUNDS = (0, 1, 7)
-Y_GROUPS = [2, 4, 2]
+P = 128
+PLACES = 4
+UNIT = 128
+UNITS = S // UNIT
+QUARTER = S // 4
+HALF = S // 2
+RUN = 4
+BANKS = 4
+EDGE = 2
 
 
-def groups(counts):
+def scalar_third(columns):
+    return columns // 3 // 16 * 16
+
+
+X_PIECES = [
+    (0, 0, T // 2, T // 2),
+    (0, T // 2, T // 2, scalar_third(T // 2)),
+    (1, 0, T // 2, T // 2),
+    (1, T // 2, T // 4, 0),
+    (1, 3 * T // 4, T // 4, scalar_third(T // 4)),
+]
+POS_LOADS = [1, 1, 2, 4]
+H_GROUPS = [2] * ((UNITS - EDGE) // 2) + [1] * EDGE
+OUT_GROUPS = [EDGE, UNITS - 2 * EDGE, EDGE]
+SCALAR_ROUNDS = list(range(EDGE)) + [UNITS - 1]
+
+
+def spans(counts):
     where = []
-    first = 0
-    for g, count in enumerate(counts):
-        for a in range(count):
-            where.append((g, a, count, first))
-        first = first + count
+    first_unit = 0
+    for group, count in enumerate(counts):
+        for nth in range(count):
+            where.append((group, nth, count, first_unit))
+        first_unit = first_unit + count
     return where
 
 
 def tile_picked_embpos_none_lo_kernel(tc, xT, w1, w2, pos, offs, out_0, out_1, out_2):
     nc = tc.nc
-    n_units = S // UNIT
     with ExitStack() as ctx:
         keep = ctx.enter_context(tc.tile_pool(name="keep", bufs=1))
-        ps1 = ctx.enter_context(tc.psum_pool(name="ps1", bufs=4))
-        ps2 = ctx.enter_context(tc.psum_pool(name="ps2", bufs=4))
+        psum_h = ctx.enter_context(tc.psum_pool(name="psum_h", bufs=BANKS))
+        psum_out = ctx.enter_context(tc.psum_pool(name="psum_out", bufs=BANKS))
 
-        x_rows = xT.rearrange("(p j) t -> p j t", j=PACK)
-        pos_rows = pos.rearrange("(p j) s -> p j s", j=PACK)
-        out_rows = out_0.rearrange("(p j) s -> p j s", j=PACK)
-        out_words = out_1.rearrange("z p c r -> p (z c r)").bitcast(I32)
-        out_scales = out_2.rearrange("z q c -> (z q) c").bitcast(I32)
+        def by_place(matrix):
+            return matrix.rearrange("(p j) n -> p j n", j=PLACES)
+
+        def unit_cols(start_unit, count=1):
+            return slice(start_unit * UNIT, (start_unit + count) * UNIT)
 
         offsets = keep.tile([P, S // 16], U16, name="offsets")
-
         x_raw = []
-        for i, (u, c0, width, share) in enumerate(X_PIECES):
+        for i, (u, first_col, width, scalar_share) in enumerate(X_PIECES):
             raw = keep.tile([P, 2, width], F32, name=f"x_raw{i}", align_bytes=64)
-            nc.sync.dma_start(out=raw[:], in_=x_rows[:, 2 * u : 2 * u + 2, c0 : c0 + width])
+            nc.sync.dma_start(out=raw[:], in_=by_place(xT)[:, 2 * u : 2 * u + 2, first_col : first_col + width])
             x_raw.append(raw)
             if i == 0:
                 nc.sync.dma_start(offsets[:], offs)
 
-        def load_w(w, tag):
-            rows = w.rearrange("(p j) c -> p j c", j=PACK)
-            halves = []
-            for a in range(2):
-                raw = keep.tile([P, PACK, H // 2], F32, name=f"{tag}{a}", tag=f"{tag}{a}", align_bytes=64)
-                nc.sync.dma_start(out=raw[:], in_=rows[:, :, a * (H // 2) : (a + 1) * (H // 2)])
-                halves.append(raw)
-            return halves
+        def load_weights(w, name):
+            width = H // 2
+            tiles = []
+            for side in range(2):
+                raw = keep.tile([P, PLACES, width], F32, name=f"{name}{side}", tag=f"{name}{side}", align_bytes=64)
+                nc.sync.dma_start(out=raw[:], in_=by_place(w)[:, :, side * width : (side + 1) * width])
+                tiles.append(raw)
+            return tiles
 
-        w1_raw = load_w(w1, "w1_raw")
-        w2_raw = load_w(w2, "w2_raw")
-        pos_sb = []
-        for g, a, count, first in groups(POS_UNITS):
-            if a == 0:
-                pos_tile = keep.tile([P, PACK, count * UNIT], F32, name=f"pos{g}", align_bytes=64)
-                nc.sync.dma_start(out=pos_tile[:], in_=pos_rows[:, :, first * UNIT : (first + count) * UNIT])
-            pos_sb.append(pos_tile[:, :, a * UNIT : (a + 1) * UNIT])
+        w1_raw = load_weights(w1, "w1_raw")
+        w2_raw = load_weights(w2, "w2_raw")
+        pos_units = []
+        for group, nth, count, first_unit in spans(POS_LOADS):
+            if nth == 0:
+                pos_tile = keep.tile([P, PLACES, count * UNIT], F32, name=f"pos{group}", align_bytes=64)
+                nc.sync.dma_start(out=pos_tile[:], in_=by_place(pos)[:, :, unit_cols(first_unit, count)])
+            pos_units.append(pos_tile[:, :, unit_cols(nth)])
+
+        def in_runs(planes):
+            return planes.rearrange("p t (c i) -> p c t i", i=RUN)
+
+        def as_words(values):
+            return values.rearrange("p (c i) t -> p c t i", i=RUN)
 
         pairs = [keep.tile([P, T], U32, name=f"pairs{u}", align_bytes=64) for u in range(2)]
-        x_words = [keep.tile([P, 256, 2], U32, name=f"x_words{c}", align_bytes=64) for c in range(2)]
-        x_planes = keep.tile([P, 2, 512], U32, name="x_planes", align_bytes=64)
+        x_quarters = [keep.tile([P, QUARTER, 2], U32, name=f"x_quarter{c}", align_bytes=64) for c in range(2)]
+        x_runs = keep.tile([P, 2, HALF], U32, name="x_runs", align_bytes=64)
 
-        def cast_pairs(copy, u, raw, c0, a, b):
-            dst = pairs[u][:, c0 + a : c0 + b].bitcast(BF16).rearrange("p (c i e) -> p c e i", i=RUN, e=2)
-            src = raw[:, :, a:b].rearrange("p e (c i) -> p c e i", i=RUN)
-            copy(out=dst, in_=src)
+        def cast_pairs(copy, u, raw, first_col, start, stop):
+            dst = pairs[u][:, first_col + start : first_col + stop].bitcast(BF16).rearrange("p (n e) -> p n e", e=2)
+            copy(out=as_words(dst), in_=in_runs(raw[:, :, start:stop]))
 
-        def gather(u, c):
-            first, count = X_CHUNKS[c]
-            cols = slice(first // 16, (first + count) // 16)
-            dst = x_words[c][:, :, u] if c < 2 else x_planes[:, u, :]
+        def gather(dst, u, first_entry, entries):
+            cols = slice(first_entry // 16, (first_entry + entries) // 16)
             nc.vector.tensor_copy(dst, pairs[u][:].indirect(offsets[:, cols]))
 
-        for i, (u, c0, width, share) in enumerate(X_PIECES):
-            if share > 0:
-                cast_pairs(nc.scalar.copy, u, x_raw[i], c0, 0, share)
-            if share < width:
-                cast_pairs(nc.vector.tensor_copy, u, x_raw[i], c0, share, width)
-            if u == 0 and c0 + width == T:
-                for c in range(3):
-                    gather(0, c)
+        def gather_quarter(u, c):
+            gather(x_quarters[c][:, :, u], u, c * QUARTER, QUARTER)
 
-        def quantize(name, src, width, tag=""):
-            codes = keep.tile([P, width], U32, name=f"{name}_codes", tag=tag, align_bytes=64)
+        def gather_half(u):
+            gather(x_runs[:, u, :], u, HALF, HALF)
+
+        for i, (u, first_col, width, scalar_share) in enumerate(X_PIECES):
+            if scalar_share > 0:
+                cast_pairs(nc.scalar.copy, u, x_raw[i], first_col, 0, scalar_share)
+            if scalar_share < width:
+                cast_pairs(nc.vector.tensor_copy, u, x_raw[i], first_col, scalar_share, width)
+            if u == 0 and first_col + width == T:
+                gather_quarter(0, 0)
+                gather_quarter(0, 1)
+                gather_half(0)
+
+        def quantize(name, src, width, codes_tag=""):
+            codes = keep.tile([P, width], U32, name=f"{name}_codes", tag=codes_tag, align_bytes=64)
             scales = keep.tile([P, width], U8, name=f"{name}_scales", align_bytes=64)
             nc.vector.quantize_mx(out=codes[:].bitcast(FP8X4), scales=scales[:], in_=src)
             return codes, scales
 
-        def deal_w(raw, tag):
-            dealt = keep.tile([P, PACK, P, PACK], BF16, name=tag, tag=tag, align_bytes=64)
-            for a in range(2):
+        def deal(raw_tiles, name):
+            dealt = keep.tile([P, PLACES, P, PLACES], BF16, name=name, tag=name, align_bytes=64)
+            for side, raw in enumerate(raw_tiles):
                 nc.scalar.copy(
-                    out=dealt[:, :, a * (P // 2) : (a + 1) * (P // 2), :].rearrange("p t m j -> p m j t"),
-                    in_=raw[a][:].rearrange("p j (m t) -> p m j t", t=PACK),
+                    out=dealt[:, :, side * (P // 2) : (side + 1) * (P // 2), :].rearrange("p t m j -> p m j t"),
+                    in_=raw[:].rearrange("p j (m t) -> p m j t", t=PLACES),
                 )
             return dealt[:].rearrange("p t m j -> p (t m j)")
 
-        def product(bank, w_q, x_q, cols):
-            for t in range(PACK):
-                m = slice(t * P, (t + 1) * P)
+        def pairs_as_values(words):
+            return words[:].rearrange("p n u -> p (n u)").bitcast(BF16)
+
+        w1_dealt = deal(w1_raw, "w1_dealt")
+        w2_dealt = deal(w2_raw, "w2_dealt")
+
+        out_codes = keep.tile([P, S], U32, name="out_codes", align_bytes=64)
+        out_scales = keep.tile([P, S], U8, name="out_scales", align_bytes=64)
+
+        gather_quarter(1, 0)
+        gather_quarter(1, 1)
+        x_q = [quantize("x0", pairs_as_values(x_quarters[0]), QUARTER)]
+        w1_q = quantize("w1", w1_dealt, H)
+        gather_half(1)
+        x_q.append(quantize("x1", pairs_as_values(x_quarters[1]), QUARTER, "w1_dealt"))
+        x_half = keep.tile([P, HALF, 2], U32, name="x_half", tag="w2_raw1", align_bytes=64)
+        nc.scalar.copy(out=as_words(x_half[:]), in_=in_runs(x_runs[:]))
+
+        def product(bank, weights, moving, cols):
+            for t in range(PLACES):
+                rows = slice(t * P, (t + 1) * P)
                 nc.tensor.matmul_mx(
                     out=bank[:, t, :],
-                    lhsT=w_q[0][:, m].bitcast(FP8X4),
-                    lhsT_scale=w_q[1][:, m],
-                    rhs=x_q[0][:, cols].bitcast(FP8X4),
-                    rhs_scale=x_q[1][:, cols],
+                    lhsT=weights[0][:, rows].bitcast(FP8X4),
+                    lhsT_scale=weights[1][:, rows],
+                    rhs=moving[0][:, cols].bitcast(FP8X4),
+                    rhs_scale=moving[1][:, cols],
                     start=True,
                     stop=True,
                 )
 
-        def as_bf16(words):
-            return words[:].rearrange("p n u -> p (n u)").bitcast(BF16)
+        h_at = spans(H_GROUPS)
+        out_at = spans(OUT_GROUPS)
+        out_bf16 = [
+            keep.tile([P, count * UNIT, PLACES], BF16, name=f"out_bf16_{group}", align_bytes=64)
+            for group, count in enumerate(OUT_GROUPS)
+        ]
+        x_at = spans([QUARTER // UNIT, QUARTER // UNIT, HALF // UNIT])
+        h_bf16 = {}
+        out_banks = {}
+        out_f32 = {}
 
-        w1_bf = deal_w(w1_raw, "w1_bf")
-        w2_bf = deal_w(w2_raw, "w2_bf")
-
-        y_codes = keep.tile([P, S], U32, name="y_codes", align_bytes=64)
-        y_scales = keep.tile([P, S], U8, name="y_scales", align_bytes=64)
-
-        x_q = {}
-        gather(1, 0)
-        gather(1, 1)
-        x_q[0] = quantize("x0", as_bf16(x_words[0]), 256)
-        w1_q = quantize("w1", w1_bf, H)
-        gather(1, 2)
-        x_q[1] = quantize("x1", as_bf16(x_words[1]), 256, "w1_bf")
-        woven = keep.tile([P, 512, 2], U32, name="woven", tag="w2_raw1", align_bytes=64)
-        nc.scalar.copy(
-            out=woven[:].rearrange("p (c i) u -> p c u i", i=RUN),
-            in_=x_planes[:].rearrange("p u (c i) -> p c u i", i=RUN),
-        )
-
-        h_at = groups(H_GROUPS)
-        store_at = groups(STORE_GROUPS)
-        h_bf = {}
-        h_q = {}
-        y_f32 = {}
-        y_cols = {}
-        banks = {}
-        y_at = groups(Y_GROUPS)
-        y_bf = [keep.tile([P, count * UNIT, PACK], BF16, name=f"y_bf{g}", align_bytes=64) for g, count in enumerate(Y_GROUPS)]
-
-        def layer1(n):
-            c = min(n // 2, 2)
-            a = n - 2 * c
-            bank = ps1.tile([P, PACK, UNIT], F32, name="bank1")
-            product(bank, w1_q, x_q[c], slice(a * UNIT, (a + 1) * UNIT))
-            g, a, count, first = h_at[n]
-            if a == 0:
-                h_bf[g] = keep.tile([P, count * UNIT, PACK], BF16, name=f"h_bf{g}", align_bytes=64)
+        def first_layer(n):
+            piece, nth_in_piece = x_at[n][:2]
+            bank = psum_h.tile([P, PLACES, UNIT], F32, name="bank_h")
+            product(bank, w1_q, x_q[piece], unit_cols(nth_in_piece))
+            group, nth, count, first_unit = h_at[n]
+            if nth == 0:
+                h_bf16[group] = keep.tile([P, count * UNIT, PLACES], BF16, name=f"h_bf16_{group}", align_bytes=64)
             nc.vector.tensor_tensor(
-                h_bf[g][:, a * UNIT : (a + 1) * UNIT, :].rearrange("p (c i) t -> p c t i", i=RUN),
-                bank[:].rearrange("p t (c i) -> p c t i", i=RUN),
-                pos_sb[n].rearrange("p t (c i) -> p c t i", i=RUN),
-                ADD,
+                as_words(h_bf16[group][:, unit_cols(nth), :]), in_runs(bank[:]), in_runs(pos_units[n]), ADD
             )
 
-        def layer2(n):
-            hg, ha, hcount, hfirst = h_at[n]
-            sg, sa, scount, sfirst = store_at[n]
-            if sa == 0:
-                y_f32[sg] = keep.tile([P, PACK, scount * UNIT], F32, name=f"y_f32{sg}", align_bytes=64)
-            bank = ps2.tile([P, PACK, UNIT], F32, name="bank2")
-            product(bank, w2_q, h_q[hg], slice(ha * UNIT, (ha + 1) * UNIT))
-            banks[n] = bank
-            y_cols[n] = y_f32[sg][:, :, sa * UNIT : (sa + 1) * UNIT]
-            nc.scalar.copy(out=y_cols[n], in_=bank[:])
-            if sa == scount - 1:
-                tok = slice(sfirst * UNIT, (sfirst + scount) * UNIT)
-                nc.sync.dma_start(out=out_rows[:, :, tok], in_=y_f32[sg][:])
+        def second_layer(n, h_q):
+            out_f32[n] = keep.tile([P, PLACES, UNIT], F32, name=f"out_f32_{n}", align_bytes=64)
+            out_banks[n] = psum_out.tile([P, PLACES, UNIT], F32, name="bank_out")
+            product(out_banks[n], w2_q, h_q, unit_cols(h_at[n][1]))
+            nc.scalar.copy(out=out_f32[n][:], in_=out_banks[n][:])
+            nc.sync.dma_start(out=by_place(out_0)[:, :, unit_cols(n)], in_=out_f32[n][:])
 
-        def y_round(n):
-            g, a, count, first = y_at[n]
-            dst = y_bf[g][:, a * UNIT : (a + 1) * UNIT, :]
+        def round_out(n):
+            group, nth, count, first_unit = out_at[n]
+            dst = out_bf16[group][:, unit_cols(nth), :]
             if n in SCALAR_ROUNDS:
-                nc.scalar.copy(out=dst, in_=banks[n][:].rearrange("p t n -> p n t"))
+                nc.scalar.copy(out=dst, in_=out_banks[n][:].rearrange("p t n -> p n t"))
             else:
-                nc.vector.tensor_copy(
-                    out=dst.rearrange("p (c i) t -> p c t i", i=RUN),
-                    in_=y_cols[n].rearrange("p t (c i) -> p c t i", i=RUN),
+                nc.vector.tensor_copy(out=as_words(dst), in_=in_runs(out_f32[n][:]))
+            if nth == count - 1:
+                cols = unit_cols(first_unit, count)
+                nc.vector.quantize_mx(
+                    out=out_codes[:, cols].bitcast(FP8X4),
+                    scales=out_scales[:, cols],
+                    in_=out_bf16[group][:].rearrange("p n t -> p (n t)"),
                 )
+                words_hbm = out_1.rearrange("z p c r -> p (z c r)").bitcast(I32)
+                nc.sync.dma_start(out=words_hbm[:, cols], in_=out_codes[:, cols].bitcast(I32))
 
-        def y_quant(g):
-            first = sum(Y_GROUPS[:g])
-            tok = slice(first * UNIT, (first + Y_GROUPS[g]) * UNIT)
-            nc.vector.quantize_mx(
-                out=y_codes[:, tok].bitcast(FP8X4),
-                scales=y_scales[:, tok],
-                in_=y_bf[g][:].rearrange("p n t -> p (n t)"),
+        w2_q = quantize("w2", w2_dealt, H)
+        for n in range(UNITS):
+            first_layer(n)
+            group, nth, count, first_unit = h_at[n]
+            if nth == count - 1:
+                h_q = quantize(f"h{group}", h_bf16[group][:].rearrange("p n t -> p (n t)"), count * UNIT)
+                for done in range(first_unit, first_unit + count):
+                    second_layer(done, h_q)
+            if n == EDGE - 1:
+                x_q.append(quantize("x2", pairs_as_values(x_half), HALF))
+                for done in range(EDGE):
+                    round_out(done)
+        for n in range(EDGE, UNITS):
+            round_out(n)
+
+        scales_hbm = out_2.rearrange("z q c -> (z q) c").bitcast(I32)
+        for quadrant in range(4):
+            queue = nc.sync if quadrant % 2 == 0 else nc.scalar
+            queue.dma_start(
+                out=scales_hbm[4 * quadrant : 4 * quadrant + 4, :],
+                in_=out_scales[32 * quadrant : 32 * quadrant + 4, :].bitcast(I32),
             )
-            nc.sync.dma_start(out=out_words[:, tok], in_=y_codes[:, tok].bitcast(I32))
-
-        w2_q = quantize("w2", w2_bf, H)
-        for n in range(n_units):
-            layer1(n)
-            g, a, count, first = h_at[n]
-            if a == count - 1:
-                h_q[g] = quantize(f"h{g}", h_bf[g][:].rearrange("p n t -> p (n t)"), count * UNIT)
-                for m in range(first, first + count):
-                    layer2(m)
-            if n == 1:
-                x_q[2] = quantize("x2", as_bf16(woven), 512)
-                y_round(0)
-                y_round(1)
-                y_quant(0)
-        for n in range(Y_GROUPS[0], n_units):
-            y_round(n)
-            g, a, count, first = y_at[n]
-            if a == count - 1:
-                y_quant(g)
-        for q in range(4):
-            queue = nc.sync if q % 2 == 0 else nc.scalar
-            queue.dma_start(out=out_scales[4 * q : 4 * q + 4, :], in_=y_scales[32 * q : 32 * q + 4, :].bitcast(I32))

from contextlib import ExitStack

import concourse.mybir as mybir

F32 = mybir.dt.float32
BF16 = mybir.dt.bfloat16
U32 = mybir.dt.uint32
I32 = mybir.dt.int32
U16 = mybir.dt.uint16
U8 = mybir.dt.uint8
FP8X4 = mybir.dt.float8_e4m3fn_x4
ADD = mybir.AluOpType.add

K, T, S, H = 512, 2048, 1024, 512
FLOPS = 2 * K * H * S + 2 * H * H * S

P = 128
PLACES = 4
UNIT = 128
UNITS = S // UNIT
QUARTER = S // 4
HALF = S // 2
RUN = 4
BANKS = 4
EDGE = 2


def scalar_third(columns):
    return columns // 3 // 16 * 16


X_PIECES = [
    (0, 0, T // 2, T // 2),
    (0, T // 2, T // 2, scalar_third(T // 2)),
    (1, 0, T // 2, T // 2),
    (1, T // 2, T // 4, 0),
    (1, 3 * T // 4, T // 4, scalar_third(T // 4)),
]
POS_LOADS = [1, 1, 2, 4]
H_GROUPS = [2] * ((UNITS - EDGE) // 2) + [1] * EDGE
OUT_GROUPS = [EDGE, UNITS - 2 * EDGE, EDGE]
SCALAR_ROUNDS = list(range(EDGE)) + [UNITS - 1]


def spans(counts):
    where = []
    first_unit = 0
    for group, count in enumerate(counts):
        for nth in range(count):
            where.append((group, nth, count, first_unit))
        first_unit = first_unit + count
    return where


def tile_picked_embpos_none_lo_kernel(tc, xT, w1, w2, pos, offs, out_0, out_1, out_2):
    nc = tc.nc
    with ExitStack() as ctx:
        keep = ctx.enter_context(tc.tile_pool(name="keep", bufs=1))
        psum_h = ctx.enter_context(tc.psum_pool(name="psum_h", bufs=BANKS))
        psum_out = ctx.enter_context(tc.psum_pool(name="psum_out", bufs=BANKS))

        def by_place(matrix):
            return matrix.rearrange("(p j) n -> p j n", j=PLACES)

        def unit_cols(start_unit, count=1):
            return slice(start_unit * UNIT, (start_unit + count) * UNIT)

        offsets = keep.tile([P, S // 16], U16, name="offsets")
        x_raw = []
        for i, (u, first_col, width, scalar_share) in enumerate(X_PIECES):
            raw = keep.tile([P, 2, width], F32, name=f"x_raw{i}", align_bytes=64)
            nc.sync.dma_start(out=raw[:], in_=by_place(xT)[:, 2 * u : 2 * u + 2, first_col : first_col + width])
            x_raw.append(raw)
            if i == 0:
                nc.sync.dma_start(offsets[:], offs)

        def load_weights(w, name):
            width = H // 2
            tiles = []
            for side in range(2):
                raw = keep.tile([P, PLACES, width], F32, name=f"{name}{side}", tag=f"{name}{side}", align_bytes=64)
                nc.sync.dma_start(out=raw[:], in_=by_place(w)[:, :, side * width : (side + 1) * width])
                tiles.append(raw)
            return tiles

        w1_raw = load_weights(w1, "w1_raw")
        w2_raw = load_weights(w2, "w2_raw")
        pos_units = []
        for group, nth, count, first_unit in spans(POS_LOADS):
            if nth == 0:
                pos_tile = keep.tile([P, PLACES, count * UNIT], F32, name=f"pos{group}", align_bytes=64)
                nc.sync.dma_start(out=pos_tile[:], in_=by_place(pos)[:, :, unit_cols(first_unit, count)])
            pos_units.append(pos_tile[:, :, unit_cols(nth)])

        def in_runs(planes):
            return planes.rearrange("p t (c i) -> p c t i", i=RUN)

        def as_words(values):
            return values.rearrange("p (c i) t -> p c t i", i=RUN)

        pairs = [keep.tile([P, T], U32, name=f"pairs{u}", align_bytes=64) for u in range(2)]
        x_quarters = [keep.tile([P, QUARTER, 2], U32, name=f"x_quarter{c}", align_bytes=64) for c in range(2)]
        x_runs = keep.tile([P, 2, HALF], U32, name="x_runs", align_bytes=64)

        def cast_pairs(copy, u, raw, first_col, start, stop):
            dst = pairs[u][:, first_col + start : first_col + stop].bitcast(BF16).rearrange("p (n e) -> p n e", e=2)
            copy(out=as_words(dst), in_=in_runs(raw[:, :, start:stop]))

        def gather(dst, u, first_entry, entries):
            cols = slice(first_entry // 16, (first_entry + entries) // 16)
            nc.vector.tensor_copy(dst, pairs[u][:].indirect(offsets[:, cols]))

        def gather_quarter(u, c):
            gather(x_quarters[c][:, :, u], u, c * QUARTER, QUARTER)

        def gather_half(u):
            gather(x_runs[:, u, :], u, HALF, HALF)

        for i, (u, first_col, width, scalar_share) in enumerate(X_PIECES):
            if scalar_share > 0:
                cast_pairs(nc.scalar.copy, u, x_raw[i], first_col, 0, scalar_share)
            if scalar_share < width:
                cast_pairs(nc.vector.tensor_copy, u, x_raw[i], first_col, scalar_share, width)
            if u == 0 and first_col + width == T:
                gather_quarter(0, 0)
                gather_quarter(0, 1)
                gather_half(0)

        def quantize(name, src, width, codes_tag=""):
            codes = keep.tile([P, width], U32, name=f"{name}_codes", tag=codes_tag, align_bytes=64)
            scales = keep.tile([P, width], U8, name=f"{name}_scales", align_bytes=64)
            nc.vector.quantize_mx(out=codes[:].bitcast(FP8X4), scales=scales[:], in_=src)
            return codes, scales

        def deal(raw_tiles, name):
            dealt = keep.tile([P, PLACES, P, PLACES], BF16, name=name, tag=name, align_bytes=64)
            for side, raw in enumerate(raw_tiles):
                nc.scalar.copy(
                    out=dealt[:, :, side * (P // 2) : (side + 1) * (P // 2), :].rearrange("p t m j -> p m j t"),
                    in_=raw[:].rearrange("p j (m t) -> p m j t", t=PLACES),
                )
            return dealt[:].rearrange("p t m j -> p (t m j)")

        def pairs_as_values(words):
            return words[:].rearrange("p n u -> p (n u)").bitcast(BF16)

        w1_dealt = deal(w1_raw, "w1_dealt")
        w2_dealt = deal(w2_raw, "w2_dealt")

        out_codes = keep.tile([P, S], U32, name="out_codes", align_bytes=64)
        out_scales = keep.tile([P, S], U8, name="out_scales", align_bytes=64)

        gather_quarter(1, 0)
        gather_quarter(1, 1)
        x_q = [quantize("x0", pairs_as_values(x_quarters[0]), QUARTER)]
        w1_q = quantize("w1", w1_dealt, H)
        gather_half(1)
        x_q.append(quantize("x1", pairs_as_values(x_quarters[1]), QUARTER, "w1_dealt"))
        x_half = keep.tile([P, HALF, 2], U32, name="x_half", tag="w2_raw1", align_bytes=64)
        nc.scalar.copy(out=as_words(x_half[:]), in_=in_runs(x_runs[:]))

        def product(bank, weights, moving, cols):
            for t in range(PLACES):
                rows = slice(t * P, (t + 1) * P)
                nc.tensor.matmul_mx(
                    out=bank[:, t, :],
                    lhsT=weights[0][:, rows].bitcast(FP8X4),
                    lhsT_scale=weights[1][:, rows],
                    rhs=moving[0][:, cols].bitcast(FP8X4),
                    rhs_scale=moving[1][:, cols],
                    start=True,
                    stop=True,
                )

        h_at = spans(H_GROUPS)
        out_at = spans(OUT_GROUPS)
        out_bf16 = [
            keep.tile([P, count * UNIT, PLACES], BF16, name=f"out_bf16_{group}", align_bytes=64)
            for group, count in enumerate(OUT_GROUPS)
        ]
        x_at = spans([QUARTER // UNIT, QUARTER // UNIT, HALF // UNIT])
        h_bf16 = {}
        out_banks = {}
        out_f32 = {}

        def first_layer(n):
            piece, nth_in_piece = x_at[n][:2]
            bank = psum_h.tile([P, PLACES, UNIT], F32, name="bank_h")
            product(bank, w1_q, x_q[piece], unit_cols(nth_in_piece))
            group, nth, count, first_unit = h_at[n]
            if nth == 0:
                h_bf16[group] = keep.tile([P, count * UNIT, PLACES], BF16, name=f"h_bf16_{group}", align_bytes=64)
            nc.vector.tensor_tensor(
                as_words(h_bf16[group][:, unit_cols(nth), :]), in_runs(bank[:]), in_runs(pos_units[n]), ADD
            )

        def second_layer(n, h_q):
            out_f32[n] = keep.tile([P, PLACES, UNIT], F32, name=f"out_f32_{n}", align_bytes=64)
            out_banks[n] = psum_out.tile([P, PLACES, UNIT], F32, name="bank_out")
            product(out_banks[n], w2_q, h_q, unit_cols(h_at[n][1]))
            nc.scalar.copy(out=out_f32[n][:], in_=out_banks[n][:])
            nc.sync.dma_start(out=by_place(out_0)[:, :, unit_cols(n)], in_=out_f32[n][:])

        def round_out(n):
            group, nth, count, first_unit = out_at[n]
            dst = out_bf16[group][:, unit_cols(nth), :]
            if n in SCALAR_ROUNDS:
                nc.scalar.copy(out=dst, in_=out_banks[n][:].rearrange("p t n -> p n t"))
            else:
                nc.vector.tensor_copy(out=as_words(dst), in_=in_runs(out_f32[n][:]))
            if nth == count - 1:
                cols = unit_cols(first_unit, count)
                nc.vector.quantize_mx(
                    out=out_codes[:, cols].bitcast(FP8X4),
                    scales=out_scales[:, cols],
                    in_=out_bf16[group][:].rearrange("p n t -> p (n t)"),
                )
                words_hbm = out_1.rearrange("z p c r -> p (z c r)").bitcast(I32)
                nc.sync.dma_start(out=words_hbm[:, cols], in_=out_codes[:, cols].bitcast(I32))

        w2_q = quantize("w2", w2_dealt, H)
        for n in range(UNITS):
            first_layer(n)
            group, nth, count, first_unit = h_at[n]
            if nth == count - 1:
                h_q = quantize(f"h{group}", h_bf16[group][:].rearrange("p n t -> p (n t)"), count * UNIT)
                for done in range(first_unit, first_unit + count):
                    second_layer(done, h_q)
            if n == EDGE - 1:
                x_q.append(quantize("x2", pairs_as_values(x_half), HALF))
                for done in range(EDGE):
                    round_out(done)
        for n in range(EDGE, UNITS):
            round_out(n)

        scales_hbm = out_2.rearrange("z q c -> (z q) c").bitcast(I32)
        for quadrant in range(4):
            queue = nc.sync if quadrant % 2 == 0 else nc.scalar
            queue.dma_start(
                out=scales_hbm[4 * quadrant : 4 * quadrant + 4, :],
                in_=out_scales[32 * quadrant : 32 * quadrant + 4, :].bitcast(I32),
            )
